import numpy as np
import ml_dtypes


def mxq(x, axis, fmt="e4m3"):
    dtype, down = {"e4m3": (ml_dtypes.float8_e4m3fn, 7), "e5m2": (ml_dtypes.float8_e5m2, 14)}[fmt]
    v = np.moveaxis(np.asarray(x, np.float32).astype(ml_dtypes.bfloat16).astype(np.float64), axis, -1)
    blocks = v.reshape(v.shape[:-1] + (-1, 32))
    amax = np.abs(blocks).max(-1, keepdims=True)
    byte = np.maximum(np.where(amax > 0, np.frexp(amax)[1] - 1 + 127, 0) - down, 1)
    scale = np.exp2(byte - 127.0)
    codes = (blocks / scale).astype(np.float32).astype(dtype).astype(np.float64)
    return np.moveaxis((codes * scale).reshape(v.shape), -1, axis)


WIDE = False


def mx_kscale(k):
    if not WIDE:
        return np.ones(k)
    levels = np.array([30, -30])
    if k % 512:
        return np.exp2(np.random.permutation(np.resize(levels, k // 32))).repeat(32)
    a = np.empty((k // 512, 16))
    for p in range(k // 512):
        a[p, :8] = np.random.permutation(np.resize(levels, 8))
        for g in range(8):
            far = levels[np.abs(levels - a[p, g]) >= 10]
            a[p, g + 8] = far[np.random.randint(len(far))]
    return np.exp2(a.ravel()).repeat(32)


def f64(x):
    return np.asarray(x).astype(np.float64)


def striped(idx):
    return np.tile(np.asarray(idx).reshape(-1, 16).T, (8, 1)).astype(np.uint16)


def unstriped(offs):
    return offs[:16].T.reshape(-1).astype(np.int64)


E2M1 = np.array([0.0, 0.5, 1.0, 1.5, 2.0, 3.0, 4.0, 6.0, -0.0, -0.5, -1.0, -1.5, -2.0, -3.0, -4.0, -6.0])


def pack_weight(w, fmt):
    k, n = w.shape
    w = f64(np.asarray(w, np.float32).astype(ml_dtypes.bfloat16)).reshape(k // 32, 32, n)
    amax = np.abs(w).max(1)
    if fmt == "e4m3":
        byte = np.frexp(amax)[1] - 1 + 127 - 7
    else:
        mant, ex = np.frexp(amax / 6.0)
        byte = np.where(mant > 0.5, ex, ex - 1) + 127
    byte = np.clip(np.where(amax > 0, byte, 1), 1, 254)
    scaled = (w * np.exp2(127.0 - byte)[:, None, :]).reshape(k, n).astype(np.float32)
    by_word = np.ascontiguousarray(scaled.reshape(k // 512, 128, 4, n).transpose(0, 1, 3, 2))
    if fmt == "e4m3":
        words = by_word.astype(ml_dtypes.float8_e4m3fn).view(np.uint8)
    else:
        c = by_word.astype(ml_dtypes.float4_e2m1fn).view(np.uint8) & 0xF
        words = (c[..., 0::2] | (c[..., 1::2] << 4)).reshape(k // 512, 128, 2 * n)
    return np.ascontiguousarray(words), np.ascontiguousarray(byte.astype(np.uint8).reshape(k // 512, 16, n))


def unpack_weight(words, scales, fmt):
    g, _, n = scales.shape
    words = np.ascontiguousarray(words).reshape(g, 128, n, -1)
    if fmt == "e4m3":
        vals = words.view(ml_dtypes.float8_e4m3fn).astype(np.float64)
    else:
        nib = np.empty((g, 128, n, 4), np.uint8)
        nib[..., 0::2] = words & 0xF
        nib[..., 1::2] = words >> 4
        vals = E2M1[nib]
    vals = vals * np.repeat(np.exp2(scales.astype(np.float64) - 127.0), 8, axis=1)[..., None]
    return vals.transpose(0, 1, 3, 2).reshape(g * 512, n)


K, T, J, I, S, C = 1024, 1024, 256, 256, 512, 512


def setup_inputs():
    n = np.random.standard_normal
    idx = np.random.permutation(T)[:J]
    idx2 = np.random.permutation(S)[:J]
    idx3 = np.random.permutation(C)[:I]
    fk = mx_kscale(K)
    kyp = pack_weight(n((K, I)) / fk[:, None], "e4m3")
    return {
        "xf": (n((K, T)) * 0.03).astype(np.float32),
        "xb": (n((K, S))).astype(np.float32),
        "fk": (np.random.uniform(0.5, 2.0, (K, 1)) * fk[:, None]).astype(np.float32),
        "ky_words": kyp[0],
        "ky_scales": kyp[1],
        "bi": (np.random.uniform(-0.7, 0.7, (1, I))).astype(np.float32),
        "tb": (1.0 * n((J, C))).astype(np.float32),
        "offs": striped(idx),
        "offs2": striped(idx2),
        "offs3": striped(idx3),
    }


def reference(xf, xb, fk, ky_words, ky_scales, bi, tb, offs, offs2, offs3):
    idx = unstriped(offs)
    idx2 = unstriped(offs2)
    idx3 = unstriped(offs3)
    kyu = unpack_weight(ky_words, ky_scales, "e4m3")
    u = f64(xf)[:, idx] * f64(xb)[:, idx2] * f64(fk)
    uq = mxq(u, 0, "e5m2")
    a0 = uq.T @ kyu
    a = a0 + f64(bi)
    y = np.tanh(a) * f64(tb)[:, idx3]
    return y

@@ -1,0 +1,129 @@
+from contextlib import ExitStack
+
+import concourse.mybir as mybir
+from concourse.masks import make_identity
+
+K, T, J, I, S, C = 1024, 1024, 256, 256, 512, 512
+FLOPS = 2 * K * J * I
+
+F32 = mybir.dt.float32
+BF16 = mybir.dt.bfloat16
+I32 = mybir.dt.int32
+U32 = mybir.dt.uint32
+U16 = mybir.dt.uint16
+U8 = mybir.dt.uint8
+E4M3 = mybir.dt.float8_e4m3fn_x4
+E5M2 = mybir.dt.float8_e5m2_x4
+MULT = mybir.AluOpType.mult
+ADD = mybir.AluOpType.add
+COPY = mybir.ActivationFunctionType.Copy
+TANH = mybir.ActivationFunctionType.Tanh
+
+P = 128
+PACK = 4
+K_PASS = P * PACK
+PASSES = K // K_PASS
+HALVES = J // P
+LIST_COLS = P // 16
+
+
+def tile_list_scores_products_given_tabled_kernel(tc, xf, xb, fk, ky_words, ky_scales, bi, tb, offs, offs2, offs3, out):
+    nc = tc.nc
+    with ExitStack() as ctx:
+        keep = ctx.enter_context(tc.tile_pool(name="keep", bufs=1))
+        psum = ctx.enter_context(tc.psum_pool(name="psum", bufs=1))
+
+        xf_list = keep.tile([P, J // 16], U16, name="xf_list")
+        xb_list = keep.tile([P, J // 16], U16, name="xb_list")
+        tb_list = keep.tile([P, I // 16], U16, name="tb_list")
+        fk_cols = keep.tile([P, PASSES, PACK], F32, name="fk_cols")
+        bi_cols = keep.tile([P, HALVES], F32, name="bi_cols")
+        xb_rows = [keep.tile([P, PACK * S], F32, name=f"xb_rows{a}") for a in range(PASSES)]
+        xf_rows = [[keep.tile([P, T], F32, name=f"xf_rows{a}_{t}") for t in range(PACK)] for a in range(PASSES)]
+        tb_rows = [keep.tile([P, C], F32, name=f"tb_rows{h}") for h in range(HALVES)]
+        ky_codes = keep.tile([P, PASSES, I], I32, name="ky_codes", align_bytes=64)
+        ky_plane = keep.tile([P, PASSES, I], U8, name="ky_plane", align_bytes=64)
+
+        def load_xb(a):
+            nc.sync.dma_start(xb_rows[a][:], xb[a * K_PASS : (a + 1) * K_PASS, :].rearrange("(p t) s -> p (t s)", t=PACK))
+
+        def load_xf(a, t):
+            nc.sync.dma_start(xf_rows[a][t][:], xf[a * K_PASS : (a + 1) * K_PASS, :].rearrange("(p t) c -> t p c", t=PACK)[t])
+
+        load_xb(0)
+        nc.sync.dma_start(xb_list[:], offs2)
+        nc.sync.dma_start(fk_cols[:], fk.rearrange("(a p t) o -> p a (t o)", a=PASSES, t=PACK))
+        nc.sync.dma_start(xf_list[:], offs)
+        for t in range(PACK):
+            load_xf(0, t)
+        load_xb(1)
+        nc.sync.dma_start(bi_cols[:], bi.rearrange("o (p m) -> (o p) m", m=HALVES))
+        nc.sync.dma_start(tb_list[:], offs3)
+        for t in range(PACK):
+            load_xf(1, t)
+        nc.sync.dma_start(ky_codes[:], ky_words.rearrange("z p c r -> p z (c r)").bitcast(I32))
+        for h in range(HALVES):
+            nc.sync.dma_start(tb_rows[h][:], tb[h * P : (h + 1) * P, :])
+
+        nc.gpsimd.memset(ky_plane[:].bitcast(I32), 0)
+        for q in range(4):
+            nc.gpsimd.dma_start(
+                ky_plane[32 * q : 32 * q + 4, :, :].bitcast(I32),
+                ky_scales[:, 4 * q : 4 * q + 4, :].rearrange("z r c -> r z c").bitcast(I32),
+            )
+        ident = keep.tile([P, P], F32, name="ident")
+        make_identity(nc, ident[:])
+
+        bias_bank = psum.tile([P, HALVES, P], F32, name="bias_bank")
+        for m in range(HALVES):
+            nc.tensor.transpose(bias_bank[:, m, :], bi_cols[:, m : m + 1].to_broadcast([P, P]), ident[:])
+        bias = keep.tile([P, P, HALVES], F32, name="bias")
+        nc.scalar.copy(bias[:], bias_bank[:].rearrange("j m p -> j p m"))
+
+        acc = [psum.tile([P, I], F32, name=f"acc{h}") for h in range(HALVES)]
+        for a in range(PASSES):
+            u = [keep.tile([P, PACK, P], F32, name=f"u{a}_{h}") for h in range(HALVES)]
+            for t in range(PACK):
+                xb_picked = keep.tile([P, J], F32, name="xb_picked", bufs=2)
+                nc.scalar.activation(xb_picked[:], xb_rows[a][:, t * S : (t + 1) * S].indirect(xb_list[:]), COPY)
+                xb_scaled = keep.tile([P, J], F32, name=f"xb_scaled{a}_{t}")
+                nc.scalar.activation(xb_scaled[:], xb_picked[:], COPY, scale=fk_cols[:, a, t : t + 1])
+                for h in range(HALVES):
+                    nc.vector.tensor_tensor(
+                        u[h][:, t, :],
+                        xf_rows[a][t][:].indirect(xf_list[:, h * LIST_COLS : (h + 1) * LIST_COLS]),
+                        xb_scaled[:, h * P : (h + 1) * P],
+                        MULT,
+                    )
+            grouped = [keep.tile([P, P, PACK], BF16, name=f"grouped{a}_{h}", align_bytes=64) for h in range(HALVES)]
+            for h in range(HALVES):
+                nc.vector.tensor_copy(
+                    grouped[h][:].rearrange("p (c i) t -> p c t i", i=4),
+                    u[h][:].rearrange("p t (c i) -> p c t i", i=4),
+                )
+            for h in range(HALVES):
+                u_codes = keep.tile([P, P], U32, name=f"u_codes{a}_{h}", align_bytes=64)
+                u_plane = keep.tile([P, P], U8, name=f"u_plane{a}_{h}", align_bytes=64)
+                nc.vector.quantize_mx(u_codes[:].bitcast(E5M2), u_plane[:], grouped[h][:].rearrange("p j t -> p (j t)"))
+                nc.tensor.matmul_mx(
+                    acc[h][:],
+                    lhsT=u_codes[:].bitcast(E5M2),
+                    lhsT_scale=u_plane[:],
+                    rhs=ky_codes[:, a, :].bitcast(E4M3),
+                    rhs_scale=ky_plane[:, a, :],
+                    start=(a == 0),
+                    stop=(a == PASSES - 1),
+                )
+
+        tb_picked = [keep.tile([P, I], F32, name=f"tb_picked{h}") for h in range(HALVES)]
+        for h in range(HALVES):
+            nc.scalar.activation(tb_picked[h][:], tb_rows[h][:].indirect(tb_list[:]), COPY)
+        score = [keep.tile([P, I], F32, name=f"score{h}") for h in range(HALVES)]
+        for h in range(HALVES):
+            nc.vector.tensor_tensor(score[h][:], acc[h][:], bias[:].rearrange("j p m -> j (p m)"), ADD)
+        for h in range(HALVES):
+            squashed = keep.tile([P, I], F32, name=f"squashed{h}")
+            nc.scalar.activation(squashed[:], score[h][:], TANH)
+            result = keep.tile([P, I], F32, name=f"result{h}")
+            nc.vector.tensor_tensor(result[:], squashed[:], tb_picked[h][:], MULT)
+            nc.sync.dma_start(out[h * P : (h + 1) * P, :], result[:])

@@ -38,69 +38,76 @@ def tile_list_scores_products_given_tabled_kernel(tc, xf, xb, fk, ky_words, ky_s
         tb_list = keep.tile([P, I // 16], U16, name="tb_list")
         fk_cols = keep.tile([P, PASSES, PACK], F32, name="fk_cols")
         bi_cols = keep.tile([P, HALVES], F32, name="bi_cols")
-        xb_rows = [keep.tile([P, PACK * S], F32, name=f"xb_rows{a}") for a in range(PASSES)]
+        xb_rows = [[keep.tile([P, 2 * S], F32, name=f"xb_rows{a}_{g}") for g in range(2)] for a in range(PASSES)]
         xf_rows = [[keep.tile([P, T], F32, name=f"xf_rows{a}_{t}") for t in range(PACK)] for a in range(PASSES)]
         tb_rows = [keep.tile([P, C], F32, name=f"tb_rows{h}") for h in range(HALVES)]
-        ky_codes = keep.tile([P, PASSES, I], I32, name="ky_codes", align_bytes=64)
+        ky_codes = [keep.tile([P, I], I32, name=f"ky_codes{a}", align_bytes=64) for a in range(PASSES)]
         ky_plane = keep.tile([P, PASSES, I], U8, name="ky_plane", align_bytes=64)
 
-        def load_xb(a):
-            nc.sync.dma_start(xb_rows[a][:], xb[a * K_PASS : (a + 1) * K_PASS, :].rearrange("(p t) s -> p (t s)", t=PACK))
+        def load_xb(a, g):
+            rows = xb[a * K_PASS : (a + 1) * K_PASS, :].rearrange("(p g t) s -> g p (t s)", g=2, t=2)
+            nc.sync.dma_start(xb_rows[a][g][:], rows[g])
 
         def load_xf(a, t):
             nc.sync.dma_start(xf_rows[a][t][:], xf[a * K_PASS : (a + 1) * K_PASS, :].rearrange("(p t) c -> t p c", t=PACK)[t])
 
-        load_xb(0)
+        load_xb(0, 0)
         nc.sync.dma_start(xb_list[:], offs2)
         nc.sync.dma_start(fk_cols[:], fk.rearrange("(a p t) o -> p a (t o)", a=PASSES, t=PACK))
+        load_xf(0, 0)
         nc.sync.dma_start(xf_list[:], offs)
-        for t in range(PACK):
-            load_xf(0, t)
-        load_xb(1)
+        load_xf(0, 1)
+        load_xb(0, 1)
+        load_xf(0, 2)
         nc.sync.dma_start(bi_cols[:], bi.rearrange("o (p m) -> (o p) m", m=HALVES))
+        load_xf(0, 3)
+        load_xb(1, 0)
+        load_xf(1, 0)
+        load_xb(1, 1)
         nc.sync.dma_start(tb_list[:], offs3)
-        for t in range(PACK):
+        for t in range(1, PACK):
             load_xf(1, t)
-        nc.sync.dma_start(ky_codes[:], ky_words.rearrange("z p c r -> p z (c r)").bitcast(I32))
         for h in range(HALVES):
+            nc.sync.dma_start(ky_codes[h][:], ky_words[h].rearrange("p c r -> p (c r)").bitcast(I32))
             nc.sync.dma_start(tb_rows[h][:], tb[h * P : (h + 1) * P, :])
 
+        ident = keep.tile([P, P], F32, name="ident")
+        make_identity(nc, ident[:])
         nc.gpsimd.memset(ky_plane[:].bitcast(I32), 0)
         for q in range(4):
             nc.gpsimd.dma_start(
                 ky_plane[32 * q : 32 * q + 4, :, :].bitcast(I32),
                 ky_scales[:, 4 * q : 4 * q + 4, :].rearrange("z r c -> r z c").bitcast(I32),
             )
-        ident = keep.tile([P, P], F32, name="ident")
-        make_identity(nc, ident[:])
 
         bias_bank = psum.tile([P, HALVES, P], F32, name="bias_bank")
         for m in range(HALVES):
             nc.tensor.transpose(bias_bank[:, m, :], bi_cols[:, m : m + 1].to_broadcast([P, P]), ident[:])
         bias = keep.tile([P, P, HALVES], F32, name="bias")
-        nc.scalar.copy(bias[:], bias_bank[:].rearrange("j m p -> j p m"))
+        nc.vector.tensor_copy(bias[:], bias_bank[:].rearrange("j m p -> j p m"))
 
         acc = [psum.tile([P, I], F32, name=f"acc{h}") for h in range(HALVES)]
         for a in range(PASSES):
-            u = [keep.tile([P, PACK, P], F32, name=f"u{a}_{h}") for h in range(HALVES)]
+            u = keep.tile([P, PACK, J], F32, name=f"u{a}")
+            grouped = [keep.tile([P, P, PACK], BF16, name=f"grouped{a}_{h}", align_bytes=64) for h in range(HALVES)]
             for t in range(PACK):
-                xb_picked = keep.tile([P, J], F32, name="xb_picked", bufs=2)
-                nc.scalar.activation(xb_picked[:], xb_rows[a][:, t * S : (t + 1) * S].indirect(xb_list[:]), COPY)
+                xb_picked = keep.tile([P, J], F32, name=f"xb_picked{a}_{t}")
+                nc.scalar.activation(xb_picked[:], xb_rows[a][t // 2][:, (t % 2) * S : (t % 2 + 1) * S].indirect(xb_list[:]), COPY)
                 xb_scaled = keep.tile([P, J], F32, name=f"xb_scaled{a}_{t}")
                 nc.scalar.activation(xb_scaled[:], xb_picked[:], COPY, scale=fk_cols[:, a, t : t + 1])
-                for h in range(HALVES):
-                    nc.vector.tensor_tensor(
-                        u[h][:, t, :],
-                        xf_rows[a][t][:].indirect(xf_list[:, h * LIST_COLS : (h + 1) * LIST_COLS]),
-                        xb_scaled[:, h * P : (h + 1) * P],
-                        MULT,
-                    )
-            grouped = [keep.tile([P, P, PACK], BF16, name=f"grouped{a}_{h}", align_bytes=64) for h in range(HALVES)]
-            for h in range(HALVES):
-                nc.vector.tensor_copy(
-                    grouped[h][:].rearrange("p (c i) t -> p c t i", i=4),
-                    u[h][:].rearrange("p t (c i) -> p c t i", i=4),
-                )
+                if (a, t) == (PASSES - 1, PACK - 1):
+                    for h in range(HALVES):
+                        cols = slice(h * P, (h + 1) * P)
+                        picked = xf_rows[a][t][:].indirect(xf_list[:, h * LIST_COLS : (h + 1) * LIST_COLS])
+                        nc.vector.tensor_tensor(u[:, t, cols], picked, xb_scaled[:, cols], MULT)
+                else:
+                    nc.vector.tensor_tensor(u[:, t, :], xf_rows[a][t][:].indirect(xf_list[:]), xb_scaled[:], MULT)
+                if t % 2 == 1:
+                    for h in range(HALVES):
+                        nc.vector.tensor_copy(
+                            grouped[h][:, :, t - 1 : t + 1].rearrange("p (c i) t -> p c t i", i=4),
+                            u[:, t - 1 : t + 1, h * P : (h + 1) * P].rearrange("p t (c i) -> p c t i", i=4),
+                        )
             for h in range(HALVES):
                 u_codes = keep.tile([P, P], U32, name=f"u_codes{a}_{h}", align_bytes=64)
                 u_plane = keep.tile([P, P], U8, name=f"u_plane{a}_{h}", align_bytes=64)
@@ -109,7 +116,7 @@ def tile_list_scores_products_given_tabled_kernel(tc, xf, xb, fk, ky_words, ky_s
                     acc[h][:],
                     lhsT=u_codes[:].bitcast(E5M2),
                     lhsT_scale=u_plane[:],
-                    rhs=ky_codes[:, a, :].bitcast(E4M3),
+                    rhs=ky_codes[a][:].bitcast(E4M3),
                     rhs_scale=ky_plane[:, a, :],
                     start=(a == 0),
                     stop=(a == PASSES - 1),

@@ -38,37 +38,33 @@ def tile_list_scores_products_given_tabled_kernel(tc, xf, xb, fk, ky_words, ky_s
         tb_list = keep.tile([P, I // 16], U16, name="tb_list")
         fk_cols = keep.tile([P, PASSES, PACK], F32, name="fk_cols")
         bi_cols = keep.tile([P, HALVES], F32, name="bi_cols")
-        xb_rows = [[keep.tile([P, 2 * S], F32, name=f"xb_rows{a}_{g}") for g in range(2)] for a in range(PASSES)]
+        xb_rows = [keep.tile([P, PACK * S], F32, name=f"xb_rows{a}") for a in range(PASSES)]
         xf_rows = [[keep.tile([P, T], F32, name=f"xf_rows{a}_{t}") for t in range(PACK)] for a in range(PASSES)]
-        tb_rows = [keep.tile([P, C], F32, name=f"tb_rows{h}") for h in range(HALVES)]
-        ky_codes = [keep.tile([P, I], I32, name=f"ky_codes{a}", align_bytes=64) for a in range(PASSES)]
+        tb_rows = [keep.tile([P, C], F32, name=f"tb_rows{h}", tag=f"tb_then_tanh{h}") for h in range(HALVES)]
+        ky_codes = keep.tile([P, PASSES, I], I32, name="ky_codes", align_bytes=64)
         ky_plane = keep.tile([P, PASSES, I], U8, name="ky_plane", align_bytes=64)
 
-        def load_xb(a, g):
-            rows = xb[a * K_PASS : (a + 1) * K_PASS, :].rearrange("(p g t) s -> g p (t s)", g=2, t=2)
-            nc.sync.dma_start(xb_rows[a][g][:], rows[g])
+        def load_xb(a):
+            nc.sync.dma_start(xb_rows[a][:], xb[a * K_PASS : (a + 1) * K_PASS, :].rearrange("(p t) s -> p (t s)", t=PACK))
 
         def load_xf(a, t):
             nc.sync.dma_start(xf_rows[a][t][:], xf[a * K_PASS : (a + 1) * K_PASS, :].rearrange("(p t) c -> t p c", t=PACK)[t])
 
-        load_xb(0, 0)
+        load_xb(0)
+        nc.scalar.dma_start(fk_cols[:], fk.rearrange("(a p t) o -> p a (t o)", a=PASSES, t=PACK))
+        nc.scalar.dma_start(bi_cols[:], bi.rearrange("o (p m) -> (o p) m", m=HALVES))
         nc.sync.dma_start(xb_list[:], offs2)
-        nc.sync.dma_start(fk_cols[:], fk.rearrange("(a p t) o -> p a (t o)", a=PASSES, t=PACK))
-        load_xf(0, 0)
         nc.sync.dma_start(xf_list[:], offs)
+        load_xf(0, 0)
         load_xf(0, 1)
-        load_xb(0, 1)
         load_xf(0, 2)
-        nc.sync.dma_start(bi_cols[:], bi.rearrange("o (p m) -> (o p) m", m=HALVES))
         load_xf(0, 3)
-        load_xb(1, 0)
-        load_xf(1, 0)
-        load_xb(1, 1)
-        nc.sync.dma_start(tb_list[:], offs3)
-        for t in range(1, PACK):
+        load_xb(1)
+        for t in range(PACK):
             load_xf(1, t)
+        nc.sync.dma_start(ky_codes[:], ky_words.rearrange("z p c r -> p z (c r)").bitcast(I32))
+        nc.sync.dma_start(tb_list[:], offs3)
         for h in range(HALVES):
-            nc.sync.dma_start(ky_codes[h][:], ky_words[h].rearrange("p c r -> p (c r)").bitcast(I32))
             nc.sync.dma_start(tb_rows[h][:], tb[h * P : (h + 1) * P, :])
 
         ident = keep.tile([P, P], F32, name="ident")
@@ -83,8 +79,8 @@ def tile_list_scores_products_given_tabled_kernel(tc, xf, xb, fk, ky_words, ky_s
         bias_bank = psum.tile([P, HALVES, P], F32, name="bias_bank")
         for m in range(HALVES):
             nc.tensor.transpose(bias_bank[:, m, :], bi_cols[:, m : m + 1].to_broadcast([P, P]), ident[:])
-        bias = keep.tile([P, P, HALVES], F32, name="bias")
-        nc.vector.tensor_copy(bias[:], bias_bank[:].rearrange("j m p -> j p m"))
+        bias = keep.tile([P, I], F32, name="bias")
+        nc.vector.tensor_copy(bias[:].rearrange("j (p m) -> j p m", m=HALVES), bias_bank[:].rearrange("j m p -> j p m"))
 
         acc = [psum.tile([P, I], F32, name=f"acc{h}") for h in range(HALVES)]
         for a in range(PASSES):
@@ -92,7 +88,7 @@ def tile_list_scores_products_given_tabled_kernel(tc, xf, xb, fk, ky_words, ky_s
             grouped = [keep.tile([P, P, PACK], BF16, name=f"grouped{a}_{h}", align_bytes=64) for h in range(HALVES)]
             for t in range(PACK):
                 xb_picked = keep.tile([P, J], F32, name=f"xb_picked{a}_{t}")
-                nc.scalar.activation(xb_picked[:], xb_rows[a][t // 2][:, (t % 2) * S : (t % 2 + 1) * S].indirect(xb_list[:]), COPY)
+                nc.scalar.activation(xb_picked[:], xb_rows[a][:, t * S : (t + 1) * S].indirect(xb_list[:]), COPY)
                 xb_scaled = keep.tile([P, J], F32, name=f"xb_scaled{a}_{t}")
                 nc.scalar.activation(xb_scaled[:], xb_picked[:], COPY, scale=fk_cols[:, a, t : t + 1])
                 if (a, t) == (PASSES - 1, PACK - 1):
@@ -116,7 +112,7 @@ def tile_list_scores_products_given_tabled_kernel(tc, xf, xb, fk, ky_words, ky_s
                     acc[h][:],
                     lhsT=u_codes[:].bitcast(E5M2),
                     lhsT_scale=u_plane[:],
-                    rhs=ky_codes[a][:].bitcast(E4M3),
+                    rhs=ky_codes[:, a, :].bitcast(E4M3),
                     rhs_scale=ky_plane[:, a, :],
                     start=(a == 0),
                     stop=(a == PASSES - 1),
@@ -127,10 +123,10 @@ def tile_list_scores_products_given_tabled_kernel(tc, xf, xb, fk, ky_words, ky_s
             nc.scalar.activation(tb_picked[h][:], tb_rows[h][:].indirect(tb_list[:]), COPY)
         score = [keep.tile([P, I], F32, name=f"score{h}") for h in range(HALVES)]
         for h in range(HALVES):
-            nc.vector.tensor_tensor(score[h][:], acc[h][:], bias[:].rearrange("j p m -> j (p m)"), ADD)
+            nc.vector.tensor_tensor(score[h][:], acc[h][:], bias[:], ADD)
+        squashed = keep.tile([P, HALVES * I], F32, name="squashed", tag=f"tb_then_tanh{HALVES - 1}")
         for h in range(HALVES):
-            squashed = keep.tile([P, I], F32, name=f"squashed{h}")
-            nc.scalar.activation(squashed[:], score[h][:], TANH)
+            nc.scalar.activation(squashed[:, h * I : (h + 1) * I], score[h][:], TANH)
             result = keep.tile([P, I], F32, name=f"result{h}")
-            nc.vector.tensor_tensor(result[:], squashed[:], tb_picked[h][:], MULT)
+            nc.vector.tensor_tensor(result[:], squashed[:, h * I : (h + 1) * I], tb_picked[h][:], MULT)
             nc.sync.dma_start(out[h * P : (h + 1) * P, :], result[:])

@@ -60,6 +60,11 @@ def tile_list_scores_products_given_tabled_kernel(tc, xf, xb, fk, ky_words, ky_s
         load_xf(0, 2)
         load_xf(0, 3)
         load_xb(1)
+        for q in range(4):
+            nc.sync.dma_start(
+                ky_plane[32 * q : 32 * q + 4, :, :].bitcast(I32),
+                ky_scales[:, 4 * q : 4 * q + 4, :].rearrange("z r c -> r z c").bitcast(I32),
+            )
         for t in range(PACK):
             load_xf(1, t)
         nc.sync.dma_start(ky_codes[:], ky_words.rearrange("z p c r -> p z (c r)").bitcast(I32))
@@ -69,12 +74,6 @@ def tile_list_scores_products_given_tabled_kernel(tc, xf, xb, fk, ky_words, ky_s
 
         ident = keep.tile([P, P], F32, name="ident")
         make_identity(nc, ident[:])
-        nc.gpsimd.memset(ky_plane[:].bitcast(I32), 0)
-        for q in range(4):
-            nc.gpsimd.dma_start(
-                ky_plane[32 * q : 32 * q + 4, :, :].bitcast(I32),
-                ky_scales[:, 4 * q : 4 * q + 4, :].rearrange("z r c -> r z c").bitcast(I32),
-            )
 
         bias_bank = psum.tile([P, HALVES, P], F32, name="bias_bank")
         for m in range(HALVES):

from contextlib import ExitStack

import concourse.mybir as mybir
from concourse.masks import make_identity

K, T, J, I, S, C = 1024, 1024, 256, 256, 512, 512
FLOPS = 2 * K * J * I

F32 = mybir.dt.float32
BF16 = mybir.dt.bfloat16
I32 = mybir.dt.int32
U32 = mybir.dt.uint32
U16 = mybir.dt.uint16
U8 = mybir.dt.uint8
E4M3 = mybir.dt.float8_e4m3fn_x4
E5M2 = mybir.dt.float8_e5m2_x4
MULT = mybir.AluOpType.mult
ADD = mybir.AluOpType.add
COPY = mybir.ActivationFunctionType.Copy
TANH = mybir.ActivationFunctionType.Tanh

P = 128
PACK = 4
K_PASS = P * PACK
PASSES = K // K_PASS
HALVES = J // P
LIST_COLS = P // 16


def tile_list_scores_products_given_tabled_kernel(tc, xf, xb, fk, ky_words, ky_scales, bi, tb, offs, offs2, offs3, out):
    nc = tc.nc
    with ExitStack() as ctx:
        keep = ctx.enter_context(tc.tile_pool(name="keep", bufs=1))
        psum = ctx.enter_context(tc.psum_pool(name="psum", bufs=1))

        xf_list = keep.tile([P, J // 16], U16, name="xf_list")
        xb_list = keep.tile([P, J // 16], U16, name="xb_list")
        tb_list = keep.tile([P, I // 16], U16, name="tb_list")
        fk_cols = keep.tile([P, PASSES, PACK], F32, name="fk_cols")
        bi_cols = keep.tile([P, HALVES], F32, name="bi_cols")
        xb_rows = [keep.tile([P, PACK * S], F32, name=f"xb_rows{a}") for a in range(PASSES)]
        xf_rows = [[keep.tile([P, T], F32, name=f"xf_rows{a}_{t}") for t in range(PACK)] for a in range(PASSES)]
        tb_rows = [keep.tile([P, C], F32, name=f"tb_rows{h}", tag=f"tb_then_tanh{h}") for h in range(HALVES)]
        ky_codes = keep.tile([P, PASSES, I], I32, name="ky_codes", align_bytes=64)
        ky_plane = keep.tile([P, PASSES, I], U8, name="ky_plane", align_bytes=64)

        def load_xb(a):
            nc.sync.dma_start(xb_rows[a][:], xb[a * K_PASS : (a + 1) * K_PASS, :].rearrange("(p t) s -> p (t s)", t=PACK))

        def load_xf(a, t):
            nc.sync.dma_start(xf_rows[a][t][:], xf[a * K_PASS : (a + 1) * K_PASS, :].rearrange("(p t) c -> t p c", t=PACK)[t])

        load_xb(0)
        nc.scalar.dma_start(fk_cols[:], fk.rearrange("(a p t) o -> p a (t o)", a=PASSES, t=PACK))
        nc.scalar.dma_start(bi_cols[:], bi.rearrange("o (p m) -> (o p) m", m=HALVES))
        nc.sync.dma_start(xb_list[:], offs2)
        nc.sync.dma_start(xf_list[:], offs)
        load_xf(0, 0)
        load_xf(0, 1)
        load_xf(0, 2)
        load_xf(0, 3)
        load_xb(1)
        for q in range(4):
            nc.sync.dma_start(
                ky_plane[32 * q : 32 * q + 4, :, :].bitcast(I32),
                ky_scales[:, 4 * q : 4 * q + 4, :].rearrange("z r c -> r z c").bitcast(I32),
            )
        for t in range(PACK):
            load_xf(1, t)
        nc.sync.dma_start(ky_codes[:], ky_words.rearrange("z p c r -> p z (c r)").bitcast(I32))
        nc.sync.dma_start(tb_list[:], offs3)
        for h in range(HALVES):
            nc.sync.dma_start(tb_rows[h][:], tb[h * P : (h + 1) * P, :])

        ident = keep.tile([P, P], F32, name="ident")
        make_identity(nc, ident[:])

        bias_bank = psum.tile([P, HALVES, P], F32, name="bias_bank")
        for m in range(HALVES):
            nc.tensor.transpose(bias_bank[:, m, :], bi_cols[:, m : m + 1].to_broadcast([P, P]), ident[:])
        bias = keep.tile([P, I], F32, name="bias")
        nc.vector.tensor_copy(bias[:].rearrange("j (p m) -> j p m", m=HALVES), bias_bank[:].rearrange("j m p -> j p m"))

        acc = [psum.tile([P, I], F32, name=f"acc{h}") for h in range(HALVES)]
        for a in range(PASSES):
            u = keep.tile([P, PACK, J], F32, name=f"u{a}")
            grouped = [keep.tile([P, P, PACK], BF16, name=f"grouped{a}_{h}", align_bytes=64) for h in range(HALVES)]
            for t in range(PACK):
                xb_picked = keep.tile([P, J], F32, name=f"xb_picked{a}_{t}")
                nc.scalar.activation(xb_picked[:], xb_rows[a][:, t * S : (t + 1) * S].indirect(xb_list[:]), COPY)
                xb_scaled = keep.tile([P, J], F32, name=f"xb_scaled{a}_{t}")
                nc.scalar.activation(xb_scaled[:], xb_picked[:], COPY, scale=fk_cols[:, a, t : t + 1])
                if (a, t) == (PASSES - 1, PACK - 1):
                    for h in range(HALVES):
                        cols = slice(h * P, (h + 1) * P)
                        picked = xf_rows[a][t][:].indirect(xf_list[:, h * LIST_COLS : (h + 1) * LIST_COLS])
                        nc.vector.tensor_tensor(u[:, t, cols], picked, xb_scaled[:, cols], MULT)
                else:
                    nc.vector.tensor_tensor(u[:, t, :], xf_rows[a][t][:].indirect(xf_list[:]), xb_scaled[:], MULT)
                if t % 2 == 1:
                    for h in range(HALVES):
                        nc.vector.tensor_copy(
                            grouped[h][:, :, t - 1 : t + 1].rearrange("p (c i) t -> p c t i", i=4),
                            u[:, t - 1 : t + 1, h * P : (h + 1) * P].rearrange("p t (c i) -> p c t i", i=4),
                        )
            for h in range(HALVES):
                u_codes = keep.tile([P, P], U32, name=f"u_codes{a}_{h}", align_bytes=64)
                u_plane = keep.tile([P, P], U8, name=f"u_plane{a}_{h}", align_bytes=64)
                nc.vector.quantize_mx(u_codes[:].bitcast(E5M2), u_plane[:], grouped[h][:].rearrange("p j t -> p (j t)"))
                nc.tensor.matmul_mx(
                    acc[h][:],
                    lhsT=u_codes[:].bitcast(E5M2),
                    lhsT_scale=u_plane[:],
                    rhs=ky_codes[:, a, :].bitcast(E4M3),
                    rhs_scale=ky_plane[:, a, :],
                    start=(a == 0),
                    stop=(a == PASSES - 1),
                )

        tb_picked = [keep.tile([P, I], F32, name=f"tb_picked{h}") for h in range(HALVES)]
        for h in range(HALVES):
            nc.scalar.activation(tb_picked[h][:], tb_rows[h][:].indirect(tb_list[:]), COPY)
        score = [keep.tile([P, I], F32, name=f"score{h}") for h in range(HALVES)]
        for h in range(HALVES):
            nc.vector.tensor_tensor(score[h][:], acc[h][:], bias[:], ADD)
        squashed = keep.tile([P, HALVES * I], F32, name="squashed", tag=f"tb_then_tanh{HALVES - 1}")
        for h in range(HALVES):
            nc.scalar.activation(squashed[:, h * I : (h + 1) * I], score[h][:], TANH)
            result = keep.tile([P, I], F32, name=f"result{h}")
            nc.vector.tensor_tensor(result[:], squashed[:, h * I : (h + 1) * I], tb_picked[h][:], MULT)
            nc.sync.dma_start(out[h * P : (h + 1) * P, :], result[:])
